import numpy as np
import ml_dtypes


def mxq(x, axis, fmt="e4m3"):
    dtype, down = {"e4m3": (ml_dtypes.float8_e4m3fn, 7), "e5m2": (ml_dtypes.float8_e5m2, 14)}[fmt]
    v = np.moveaxis(np.asarray(x, np.float32).astype(ml_dtypes.bfloat16).astype(np.float64), axis, -1)
    blocks = v.reshape(v.shape[:-1] + (-1, 32))
    amax = np.abs(blocks).max(-1, keepdims=True)
    byte = np.maximum(np.where(amax > 0, np.frexp(amax)[1] - 1 + 127, 0) - down, 1)
    scale = np.exp2(byte - 127.0)
    codes = (blocks / scale).astype(np.float32).astype(dtype).astype(np.float64)
    return np.moveaxis((codes * scale).reshape(v.shape), -1, axis)


WIDE = False


def mx_kscale(k):
    if not WIDE:
        return np.ones(k)
    levels = np.array([10, -10, 5, -5, 0])
    if k % 512:
        return np.exp2(np.random.permutation(np.resize(levels, k // 32))).repeat(32)
    a = np.empty((k // 512, 16))
    for p in range(k // 512):
        a[p, :8] = np.random.permutation(np.resize(levels, 8))
        for g in range(8):
            far = levels[np.abs(levels - a[p, g]) >= 10]
            a[p, g + 8] = far[np.random.randint(len(far))]
    return np.exp2(a.ravel()).repeat(32)


def f64(x):
    return np.asarray(x).astype(np.float64)


def striped(idx):
    return np.tile(idx.reshape(-1, 16).T, (8, 1)).astype(np.uint16)


def unstriped(offs):
    return offs[:16].T.reshape(-1).astype(np.int64)


def pack_weight(w):
    k, n = w.shape
    w = f64(np.asarray(w, np.float32).astype(ml_dtypes.bfloat16)).reshape(k // 32, 32, n)
    amax = np.abs(w).max(1)
    byte = np.clip(np.where(amax > 0, np.frexp(amax)[1] - 1 + 127 - 7, 1), 1, 254)
    scaled = (w * np.exp2(127.0 - byte)[:, None, :]).reshape(k, n).astype(np.float32)
    words = np.ascontiguousarray(scaled.reshape(k // 512, 128, 4, n).transpose(0, 1, 3, 2)).astype(ml_dtypes.float8_e4m3fn).view(np.uint8)
    return words, np.ascontiguousarray(byte.astype(np.uint8).reshape(k // 512, 16, n))


def unpack_weight(words, scales):
    g, p, n, _ = words.shape
    vals = np.ascontiguousarray(words).view(ml_dtypes.float8_e4m3fn).astype(np.float64) * np.repeat(np.exp2(scales.astype(np.float64) - 127.0), 8, axis=1)[..., None]
    return vals.transpose(0, 1, 3, 2).reshape(g * 512, n)


def sigmoid(v):
    return 1.0 / (1.0 + np.exp(-np.maximum(v, -700.0)))


K, T, S, N, H, U = 512, 1024, 512, 256, 512, 1024
P = 2 ** 7


def setup_inputs():
    n = np.random.standard_normal
    s = mx_kscale(K)[:, None]
    u = mx_kscale(H)
    packed_xT = pack_weight(n((K, T)) * s)
    return {
        "x_words": packed_xT[0],
        "x_scales": packed_xT[1],
        "wu": (n((K, H)) / np.sqrt(K) / s).astype(np.float32),
        "wr": (n((K, H)) / np.sqrt(K) / s).astype(np.float32),
        "wh": (n((K, H)) / np.sqrt(K) / s).astype(np.float32),
        "mem": (0.7 * n((H, U))).astype(np.float32),
        "att": (np.tile(np.random.uniform(0.1, 1.0, S), (P, 1))).astype(np.float32),
        "vu": (n((H, 1))).astype(np.float32),
        "vh": (n((H, 1))).astype(np.float32),
        "unit": (np.random.uniform(0.5, 1.5, (H, 1)) * u[:, None]).astype(np.float32),
        "wo": (n((H, N)) / np.sqrt(H) / u[:, None]).astype(np.float32),
        "offs": striped(np.random.permutation(T)[:S]),
        "user": striped(np.random.permutation(U)[:S]),
    }


def reference(x_words, x_scales, wu, wr, wh, mem, att, vu, vh, unit, wo, offs, user):
    xq = unpack_weight(x_words, x_scales)[:, unstriped(offs)]
    yu = mxq(f64(wu), 0, "e4m3").T @ xq
    hid = f64(mem)[:, unstriped(user)]
    up = f64(att)[:1] * (sigmoid(yu + f64(vu) * hid))
    yh = mxq(f64(wh), 0, "e4m3").T @ xq
    yr = mxq(f64(wr), 0, "e4m3").T @ xq
    cand = np.tanh(yh + sigmoid(yr) * (f64(vh) * hid))
    hnew = (-1.0 * up + 1.0) * hid + up * cand
    hmix = hnew * np.abs(cand) + 0.3 * hid
    zz = f64(unit) * hmix
    return mxq(f64(wo), 0, "e4m3").T @ mxq(zz, 0, "e4m3")

@@ -1,0 +1,289 @@
+from contextlib import ExitStack
+
+import concourse.mybir as mybir
+from concourse.masks import make_identity
+
+K, T, S, N, H, U = 512, 1024, 512, 256, 512, 1024
+P = 128
+PACK = 4
+FLOPS = 2 * K * H * S * 3 + 2 * H * N * S
+
+F32 = mybir.dt.float32
+BF16 = mybir.dt.bfloat16
+I32 = mybir.dt.int32
+U32 = mybir.dt.uint32
+U16 = mybir.dt.uint16
+U8 = mybir.dt.uint8
+FP8X4 = mybir.dt.float8_e4m3fn_x4
+ALU = mybir.AluOpType
+ACT = mybir.ActivationFunctionType
+
+CHUNK = 128
+
+
+def tile_picked_yaugru_mix_p_kernel(
+    tc, x_words, x_scales, wu, wr, wh, mem, att, vu, vh, unit, wo, offs, user, out
+):
+    nc = tc.nc
+    with ExitStack() as ctx:
+        keep = ctx.enter_context(tc.tile_pool(name="keep", bufs=1))
+        shared = ctx.enter_context(tc.tile_pool(name="shared", bufs=1))
+        psum = ctx.enter_context(tc.psum_pool(name="psum", bufs=1))
+
+        def tenant(place, shape, dtype, name):
+            if place is None:
+                return keep.tile(shape, dtype, name=name, align_bytes=64)
+            return shared.tile(shape, dtype, name=name, align_bytes=64, offset=4096 * place)
+
+        offs_sb = keep.tile([P, S // 16], U16, name="offs_sb")
+        user_sb = keep.tile([P, S // 16], U16, name="user_sb")
+        words_all = keep.tile([P, T], I32, name="words_all")
+        bytes_all = keep.tile([P, T], U8, name="bytes_all")
+        raw = {name: keep.tile([P, PACK, H], F32, name="raw_" + name) for name in ("wr", "wh", "wu")}
+        raw_wo = keep.tile([P, PACK, N], F32, name="raw_wo")
+        mem_sb = [tenant((2, 3, None, 7)[t], [P, U], F32, "mem%d" % t) for t in range(PACK)]
+        vu_sb = keep.tile([P, PACK], F32, name="vu_sb")
+        vh_sb = keep.tile([P, PACK], F32, name="vh_sb")
+        unit_sb = keep.tile([P, PACK], F32, name="unit_sb")
+        att_sb = keep.tile([P, S // P], F32, name="att_sb")
+        ident = keep.tile([P, P], F32, name="ident")
+
+        mem_rows = mem.rearrange("(p t) u -> p t u", t=PACK)
+
+        def rows4(w):
+            return w.rearrange("(p j) c -> p j c", j=PACK)
+
+        def column4(v):
+            return v.rearrange("(p t) o -> p (t o)", t=PACK)
+
+        nc.vector.memset(bytes_all[:].bitcast(I32), 0)
+        nc.sync.dma_start(out=words_all[:], in_=x_words[0].rearrange("p c r -> p (c r)").bitcast(I32))
+        nc.sync.dma_start(offs_sb[:], offs)
+        for q in range(4):
+            nc.sync.dma_start(
+                out=bytes_all[32 * q : 32 * q + 4, :].bitcast(I32), in_=x_scales[0, 4 * q : 4 * q + 4, :].bitcast(I32)
+            )
+        nc.sync.dma_start(out=raw["wr"][:], in_=rows4(wr))
+        nc.sync.dma_start(user_sb[:], user)
+        nc.sync.dma_start(out=mem_sb[0][:], in_=mem_rows[:, 0, :])
+        nc.sync.dma_start(out=vh_sb[:], in_=column4(vh))
+        nc.sync.dma_start(out=raw["wh"][:], in_=rows4(wh))
+        nc.sync.dma_start(out=mem_sb[1][:], in_=mem_rows[:, 1, :])
+        nc.sync.dma_start(out=unit_sb[:], in_=column4(unit))
+        nc.sync.dma_start(out=raw["wu"][:], in_=rows4(wu))
+        nc.sync.dma_start(out=vu_sb[:], in_=column4(vu))
+        nc.sync.dma_start(out=mem_sb[2][:], in_=mem_rows[:, 2, :])
+        with nc.allow_non_contiguous_dma(reason="one attention value a partition"):
+            nc.sync.dma_start(out=att_sb[:], in_=att[0:1, :].rearrange("o (s p) -> p (o s)", p=P))
+        nc.sync.dma_start(out=mem_sb[3][:], in_=mem_rows[:, 3, :])
+        nc.sync.dma_start(out=raw_wo[:], in_=rows4(wo))
+        make_identity(nc, ident[:])
+
+        x_codes = keep.tile([P, S], U32, name="x_codes", align_bytes=64)
+        x_scale = keep.tile([P, S], U8, name="x_scale", align_bytes=64)
+        nc.vector.tensor_copy(out=x_codes[:], in_=words_all[:].bitcast(U32).indirect(offs_sb[:]))
+        nc.vector.tensor_copy(out=x_scale[:], in_=bytes_all[:].indirect(offs_sb[:]))
+
+        grouped, codes, scales = {}, {}, {}
+
+        def cast_weight(name, half, copy, place):
+            key = name + "ab"[half]
+            grouped[key] = tenant(place, [P, 2, P, PACK], BF16, "grouped_" + key)
+            src = raw[name][:].rearrange("p j (m t) -> p m j t", t=PACK)
+            copy(out=grouped[key][:].rearrange("p t m j -> p m j t"), in_=src[:, :, :, 2 * half : 2 * half + 2])
+
+        def quantize(name, flat, width):
+            codes[name] = keep.tile([P, width], U32, name="codes_" + name, align_bytes=64)
+            scales[name] = keep.tile([P, width], U8, name="scales_" + name, align_bytes=64)
+            nc.vector.quantize_mx(out=codes[name][:].bitcast(FP8X4), scales=scales[name][:], in_=flat)
+
+        def quantize_weight(name, half):
+            key = name + "ab"[half]
+            quantize(key, grouped[key][:].rearrange("p t m j -> p (t m j)"), H // 2)
+
+        def product(name, t):
+            bank = psum.tile([P, S], F32, name="y_%s%d" % (name, t), tag="cand" if name == "wh" else "gate", bufs=2)
+            key = name + "ab"[t // 2]
+            cols = slice(P * (t % 2), P * (t % 2 + 1))
+            nc.tensor.matmul_mx(
+                out=bank[:],
+                lhsT=codes[key][:, cols].bitcast(FP8X4),
+                lhsT_scale=scales[key][:, cols],
+                rhs=x_codes[:].bitcast(FP8X4),
+                rhs_scale=x_scale[:],
+                start=True,
+                stop=True,
+            )
+            return bank
+
+        def turned(name, tag, *terms):
+            bank = psum.tile([P, S], F32, name=name, tag=tag, bufs=2)
+            for s in range(S // P):
+                cols = slice(P * s, P * (s + 1))
+                for n, term in enumerate(terms):
+                    nc.tensor.matmul(
+                        bank[:, cols], term[:, cols], ident[:], start=(n == 0), stop=(n == len(terms) - 1), is_transpose=True
+                    )
+            return bank
+
+        def plane(name, t, place=None):
+            return tenant(place, [P, S], F32, "%s%d" % (name, t))
+
+        hid, reset, gated, neg_cand, size, diff_t, gate_t, step_t = {}, {}, {}, {}, {}, {}, {}, {}
+        scaled = {}
+        kept = keep.tile([P, PACK, S], F32, name="kept")
+        moved = keep.tile([P, PACK, S], F32, name="moved")
+
+        def reset_gate(t):
+            reset[t] = plane("reset", t, (1, None, None, None)[t])
+            nc.scalar.activation(out=reset[t][:], in_=product("wr", t)[:], func=ACT.Sigmoid)
+
+        def gather_state(t):
+            hid[t] = plane("hid", t, (0, 2, 5, 6)[t])
+            nc.vector.tensor_copy(out=hid[t][:], in_=mem_sb[t][:].indirect(user_sb[:]))
+
+        def gate_state(t):
+            gated[t] = plane("gated", t, (4, 5, 6, None)[t])
+            nc.vector.scalar_tensor_tensor(
+                out=gated[t][:], in0=hid[t][:], scalar=vh_sb[:, t : t + 1], in1=reset[t][:], op0=ALU.mult, op1=ALU.mult
+            )
+
+        def candidate(t):
+            pre = plane("cand_pre", t)
+            nc.vector.tensor_tensor(out=pre[:], in0=product("wh", t)[:], in1=gated[t][:], op=ALU.add)
+            neg_cand[t] = plane("neg_cand", t)
+            nc.scalar.activation(out=neg_cand[t][:], in_=pre[:], func=ACT.Tanh, scale=-1.0)
+            diff_t[t] = turned("diff_t%d" % t, "diff", hid[t], neg_cand[t])
+            size[t] = plane("size", t)
+            nc.scalar.activation(out=size[t][:], in_=neg_cand[t][:], func=ACT.Abs)
+            nc.scalar.activation(out=pre[:], in_=hid[t][:], func=ACT.Copy, scale=unit_sb[:, t : t + 1])
+            scaled[t] = pre
+
+        def update_gate(t):
+            pre = plane("gate_pre", t)
+            nc.vector.scalar_tensor_tensor(
+                out=pre[:], in0=hid[t][:], scalar=vu_sb[:, t : t + 1], in1=product("wu", t)[:], op0=ALU.mult, op1=ALU.add
+            )
+            gate_t[t] = plane("gate_t", t)
+            nc.scalar.activation(out=gate_t[t][:], in_=turned("gate_pre_t%d" % t, "pre", pre)[:], func=ACT.Sigmoid)
+
+        def keep_term(t):
+            nc.vector.scalar_tensor_tensor(
+                out=kept[:, t, :], in0=size[t][:], scalar=0.3, in1=scaled[t][:], op0=ALU.add, op1=ALU.mult
+            )
+
+        def step(t):
+            step_t[t] = plane("step_t", t)
+            for s in range(S // P):
+                cols = slice(P * s, P * (s + 1))
+                nc.vector.scalar_tensor_tensor(
+                    out=step_t[t][:, cols],
+                    in0=gate_t[t][:, cols],
+                    scalar=att_sb[:, s : s + 1],
+                    in1=diff_t[t][:, cols],
+                    op0=ALU.mult,
+                    op1=ALU.mult,
+                )
+
+        def move_term(t):
+            nc.vector.scalar_tensor_tensor(
+                out=moved[:, t, :],
+                in0=turned("step%d" % t, "cand", step_t[t])[:],
+                scalar=unit_sb[:, t : t + 1],
+                in1=size[t][:],
+                op0=ALU.mult,
+                op1=ALU.mult,
+            )
+
+        def cast_readout():
+            grouped["wo"] = tenant(7, [P, N, PACK], BF16, "grouped_wo")
+            nc.scalar.copy(
+                out=grouped["wo"][:].rearrange("p (c i) j -> p c j i", i=4),
+                in_=raw_wo[:].rearrange("p j (c i) -> p c j i", i=4),
+            )
+
+        zz = {}
+
+        def mix(c):
+            cols = slice(CHUNK * c, CHUNK * (c + 1))
+            zz[c] = keep.tile([P, CHUNK, PACK], BF16, name="zz%d" % c, align_bytes=64)
+            nc.vector.tensor_tensor(
+                out=zz[c][:].rearrange("p (c i) t -> p c t i", i=4),
+                in0=kept[:, :, cols].rearrange("p t (c i) -> p c t i", i=4),
+                in1=moved[:, :, cols].rearrange("p t (c i) -> p c t i", i=4),
+                op=ALU.subtract,
+            )
+
+        out_rows = out.rearrange("(a p) j -> p a j", p=P)
+
+        def read_out(c):
+            name = "zz%d" % c
+            quantize(name, zz[c][:].rearrange("p n t -> p (n t)"), CHUNK)
+            bank = psum.tile([P, N // P, CHUNK], F32, name="out%d" % c, tag="gate", bufs=2)
+            for a in range(N // P):
+                cols = slice(P * a, P * (a + 1))
+                nc.tensor.matmul_mx(
+                    out=bank[:, a, :],
+                    lhsT=codes["wo"][:, cols].bitcast(FP8X4),
+                    lhsT_scale=scales["wo"][:, cols],
+                    rhs=codes[name][:].bitcast(FP8X4),
+                    rhs_scale=scales[name][:],
+                    start=True,
+                    stop=True,
+                )
+            result = keep.tile([P, N // P, CHUNK], F32, name="result%d" % c)
+            nc.scalar.copy(out=result[:], in_=bank[:])
+            nc.sync.dma_start(out=out_rows[:, :, CHUNK * c : CHUNK * (c + 1)], in_=result[:])
+
+        cast_weight("wr", 0, nc.vector.tensor_copy, 0)
+        cast_weight("wr", 1, nc.scalar.copy, None)
+        quantize_weight("wr", 0)
+        quantize_weight("wr", 1)
+        reset_gate(0)
+        reset_gate(1)
+        gather_state(0)
+        gate_state(0)
+        cast_weight("wh", 0, nc.vector.tensor_copy, 1)
+        cast_weight("wh", 1, nc.scalar.copy, 2)
+        reset_gate(2)
+        reset_gate(3)
+        quantize_weight("wh", 0)
+        quantize_weight("wh", 1)
+        gather_state(1)
+        cast_weight("wu", 0, nc.scalar.copy, 3)
+        candidate(0)
+        cast_weight("wu", 1, nc.scalar.copy, 4)
+        gate_state(1)
+        candidate(1)
+        gather_state(2)
+        quantize_weight("wu", 0)
+        gate_state(2)
+        quantize_weight("wu", 1)
+        candidate(2)
+        update_gate(0)
+        gather_state(3)
+        update_gate(1)
+        gate_state(3)
+        keep_term(0)
+        candidate(3)
+        step(0)
+        update_gate(2)
+        keep_term(1)
+        step(1)
+        update_gate(3)
+        cast_readout()
+        move_term(0)
+        keep_term(2)
+        step(2)
+        move_term(1)
+        step(3)
+        keep_term(3)
+        move_term(2)
+        quantize("wo", grouped["wo"][:].rearrange("p n j -> p (n j)"), N)
+        move_term(3)
+        chunks = S // CHUNK
+        mix(0)
+        for c in range(chunks):
+            if c + 1 < chunks:
+                mix(c + 1)
+            read_out(c)

@@ -18,7 +18,8 @@ FP8X4 = mybir.dt.float8_e4m3fn_x4
 ALU = mybir.AluOpType
 ACT = mybir.ActivationFunctionType
 
-CHUNK = 128
+CHUNKS = (128, 128, 128, 64, 64)
+STATE_ON_TENSOR = (1, 2)
 
 
 def tile_picked_yaugru_mix_p_kernel(
@@ -26,84 +27,83 @@ def tile_picked_yaugru_mix_p_kernel(
 ):
     nc = tc.nc
     with ExitStack() as ctx:
-        keep = ctx.enter_context(tc.tile_pool(name="keep", bufs=1))
-        shared = ctx.enter_context(tc.tile_pool(name="shared", bufs=1))
+        sbuf = ctx.enter_context(tc.tile_pool(name="sbuf", bufs=1))
         psum = ctx.enter_context(tc.psum_pool(name="psum", bufs=1))
 
-        def tenant(place, shape, dtype, name):
-            if place is None:
-                return keep.tile(shape, dtype, name=name, align_bytes=64)
-            return shared.tile(shape, dtype, name=name, align_bytes=64, offset=4096 * place)
+        def aligned(shape, dtype, name):
+            return sbuf.tile(shape, dtype, name=name, align_bytes=64)
 
-        offs_sb = keep.tile([P, S // 16], U16, name="offs_sb")
-        user_sb = keep.tile([P, S // 16], U16, name="user_sb")
-        words_all = keep.tile([P, T], I32, name="words_all")
-        bytes_all = keep.tile([P, T], U8, name="bytes_all")
-        raw = {name: keep.tile([P, PACK, H], F32, name="raw_" + name) for name in ("wr", "wh", "wu")}
-        raw_wo = keep.tile([P, PACK, N], F32, name="raw_wo")
-        mem_sb = [tenant((2, 3, None, 7)[t], [P, U], F32, "mem%d" % t) for t in range(PACK)]
-        vu_sb = keep.tile([P, PACK], F32, name="vu_sb")
-        vh_sb = keep.tile([P, PACK], F32, name="vh_sb")
-        unit_sb = keep.tile([P, PACK], F32, name="unit_sb")
-        att_sb = keep.tile([P, S // P], F32, name="att_sb")
-        ident = keep.tile([P, P], F32, name="ident")
+        offs_sb = sbuf.tile([P, S // 16], U16, name="offs_sb")
+        user_sb = sbuf.tile([P, S // 16], U16, name="user_sb")
+        words_all = sbuf.tile([P, T], I32, name="words_all")
+        bytes_all = sbuf.tile([P, T], U8, name="bytes_all")
+        raw = {name: sbuf.tile([P, PACK, H], F32, name="raw_" + name) for name in ("wr", "wh", "wu")}
+        raw_wo = sbuf.tile([P, PACK, N], F32, name="raw_wo")
+        mem_sb = [aligned([P, U], F32, "mem%d" % t) for t in range(PACK)]
+        vu_sb = sbuf.tile([P, PACK], F32, name="vu_sb")
+        vh_sb = sbuf.tile([P, PACK], F32, name="vh_sb")
+        unit_sb = sbuf.tile([P, PACK], F32, name="unit_sb")
+        att_sb = sbuf.tile([P, S // P], F32, name="att_sb")
+        ident = sbuf.tile([P, P], F32, name="ident")
 
         mem_rows = mem.rearrange("(p t) u -> p t u", t=PACK)
 
-        def rows4(w):
+        def four_rows(w):
             return w.rearrange("(p j) c -> p j c", j=PACK)
 
-        def column4(v):
+        def by_plane(v):
             return v.rearrange("(p t) o -> p (t o)", t=PACK)
 
         nc.vector.memset(bytes_all[:].bitcast(I32), 0)
         nc.sync.dma_start(out=words_all[:], in_=x_words[0].rearrange("p c r -> p (c r)").bitcast(I32))
         nc.sync.dma_start(offs_sb[:], offs)
-        for q in range(4):
+        for q in range(P // 32):
             nc.sync.dma_start(
                 out=bytes_all[32 * q : 32 * q + 4, :].bitcast(I32), in_=x_scales[0, 4 * q : 4 * q + 4, :].bitcast(I32)
             )
-        nc.sync.dma_start(out=raw["wr"][:], in_=rows4(wr))
+        nc.sync.dma_start(out=raw["wr"][:], in_=four_rows(wr))
         nc.sync.dma_start(user_sb[:], user)
         nc.sync.dma_start(out=mem_sb[0][:], in_=mem_rows[:, 0, :])
-        nc.sync.dma_start(out=vh_sb[:], in_=column4(vh))
-        nc.sync.dma_start(out=raw["wh"][:], in_=rows4(wh))
+        nc.sync.dma_start(out=raw["wh"][:], in_=four_rows(wh))
         nc.sync.dma_start(out=mem_sb[1][:], in_=mem_rows[:, 1, :])
-        nc.sync.dma_start(out=unit_sb[:], in_=column4(unit))
-        nc.sync.dma_start(out=raw["wu"][:], in_=rows4(wu))
-        nc.sync.dma_start(out=vu_sb[:], in_=column4(vu))
+        nc.sync.dma_start(out=raw["wu"][:], in_=four_rows(wu))
         nc.sync.dma_start(out=mem_sb[2][:], in_=mem_rows[:, 2, :])
+        nc.sync.dma_start(out=mem_sb[3][:], in_=mem_rows[:, 3, :])
         with nc.allow_non_contiguous_dma(reason="one attention value a partition"):
             nc.sync.dma_start(out=att_sb[:], in_=att[0:1, :].rearrange("o (s p) -> p (o s)", p=P))
-        nc.sync.dma_start(out=mem_sb[3][:], in_=mem_rows[:, 3, :])
-        nc.sync.dma_start(out=raw_wo[:], in_=rows4(wo))
+        nc.sync.dma_start(out=raw_wo[:], in_=four_rows(wo))
+        nc.gpsimd.dma_start(out=vh_sb[:], in_=by_plane(vh))
+        nc.gpsimd.dma_start(out=unit_sb[:], in_=by_plane(unit))
+        nc.gpsimd.dma_start(out=vu_sb[:], in_=by_plane(vu))
         make_identity(nc, ident[:])
+        unit_03 = sbuf.tile([P, PACK], F32, name="unit_03")
+        nc.gpsimd.tensor_scalar(out=unit_03[:], in0=unit_sb[:], scalar1=0.3, scalar2=None, op0=ALU.mult)
 
-        x_codes = keep.tile([P, S], U32, name="x_codes", align_bytes=64)
-        x_scale = keep.tile([P, S], U8, name="x_scale", align_bytes=64)
+        x_codes = aligned([P, S], U32, "x_codes")
+        x_scale = aligned([P, S], U8, "x_scale")
         nc.vector.tensor_copy(out=x_codes[:], in_=words_all[:].bitcast(U32).indirect(offs_sb[:]))
         nc.vector.tensor_copy(out=x_scale[:], in_=bytes_all[:].indirect(offs_sb[:]))
 
-        grouped, codes, scales = {}, {}, {}
+        rounded, codes, scales = {}, {}, {}
 
-        def cast_weight(name, half, copy, place):
-            key = name + "ab"[half]
-            grouped[key] = tenant(place, [P, 2, P, PACK], BF16, "grouped_" + key)
+        def round_weight(name, half, copy):
+            key = "%s%d" % (name, half)
+            rounded[key] = aligned([P, 2, P, PACK], BF16, "rounded_" + key)
             src = raw[name][:].rearrange("p j (m t) -> p m j t", t=PACK)
-            copy(out=grouped[key][:].rearrange("p t m j -> p m j t"), in_=src[:, :, :, 2 * half : 2 * half + 2])
+            copy(out=rounded[key][:].rearrange("p t m j -> p m j t"), in_=src[:, :, :, 2 * half : 2 * half + 2])
 
-        def quantize(name, flat, width):
-            codes[name] = keep.tile([P, width], U32, name="codes_" + name, align_bytes=64)
-            scales[name] = keep.tile([P, width], U8, name="scales_" + name, align_bytes=64)
-            nc.vector.quantize_mx(out=codes[name][:].bitcast(FP8X4), scales=scales[name][:], in_=flat)
+        def quantize(key, flat, width):
+            codes[key] = aligned([P, width], U32, "codes_" + key)
+            scales[key] = aligned([P, width], U8, "scales_" + key)
+            nc.vector.quantize_mx(out=codes[key][:].bitcast(FP8X4), scales=scales[key][:], in_=flat)
 
         def quantize_weight(name, half):
-            key = name + "ab"[half]
-            quantize(key, grouped[key][:].rearrange("p t m j -> p (t m j)"), H // 2)
+            key = "%s%d" % (name, half)
+            quantize(key, rounded[key][:].rearrange("p t m j -> p (t m j)"), H // 2)
 
         def product(name, t):
             bank = psum.tile([P, S], F32, name="y_%s%d" % (name, t), tag="cand" if name == "wh" else "gate", bufs=2)
-            key = name + "ab"[t // 2]
+            key = "%s%d" % (name, t // 2)
             cols = slice(P * (t % 2), P * (t % 2 + 1))
             nc.tensor.matmul_mx(
                 out=bank[:],
@@ -126,53 +126,47 @@ def tile_picked_yaugru_mix_p_kernel(
                     )
             return bank
 
-        def plane(name, t, place=None):
-            return tenant(place, [P, S], F32, "%s%d" % (name, t))
+        def plane(name, t):
+            return aligned([P, S], F32, "%s%d" % (name, t))
 
-        hid, reset, gated, neg_cand, size, diff_t, gate_t, step_t = {}, {}, {}, {}, {}, {}, {}, {}
-        scaled = {}
-        kept = keep.tile([P, PACK, S], F32, name="kept")
-        moved = keep.tile([P, PACK, S], F32, name="moved")
+        hid, reset, gated, neg_cand, size, diff_t, gate_t, step_t, neg_hid_t = {}, {}, {}, {}, {}, {}, {}, {}, {}
+        kept = sbuf.tile([P, PACK, S], F32, name="kept")
+        moved = sbuf.tile([P, PACK, S], F32, name="moved")
 
         def reset_gate(t):
-            reset[t] = plane("reset", t, (1, None, None, None)[t])
+            reset[t] = plane("reset", t)
             nc.scalar.activation(out=reset[t][:], in_=product("wr", t)[:], func=ACT.Sigmoid)
 
-        def gather_state(t):
-            hid[t] = plane("hid", t, (0, 2, 5, 6)[t])
+        def candidate(t):
+            hid[t] = plane("hid", t)
             nc.vector.tensor_copy(out=hid[t][:], in_=mem_sb[t][:].indirect(user_sb[:]))
-
-        def gate_state(t):
-            gated[t] = plane("gated", t, (4, 5, 6, None)[t])
+            gated[t] = plane("gated", t)
             nc.vector.scalar_tensor_tensor(
                 out=gated[t][:], in0=hid[t][:], scalar=vh_sb[:, t : t + 1], in1=reset[t][:], op0=ALU.mult, op1=ALU.mult
             )
-
-        def candidate(t):
-            pre = plane("cand_pre", t)
-            nc.vector.tensor_tensor(out=pre[:], in0=product("wh", t)[:], in1=gated[t][:], op=ALU.add)
+            cand_pre = plane("cand_pre", t)
+            nc.vector.tensor_tensor(out=cand_pre[:], in0=product("wh", t)[:], in1=gated[t][:], op=ALU.add)
             neg_cand[t] = plane("neg_cand", t)
-            nc.scalar.activation(out=neg_cand[t][:], in_=pre[:], func=ACT.Tanh, scale=-1.0)
-            diff_t[t] = turned("diff_t%d" % t, "diff", hid[t], neg_cand[t])
-            size[t] = plane("size", t)
-            nc.scalar.activation(out=size[t][:], in_=neg_cand[t][:], func=ACT.Abs)
-            nc.scalar.activation(out=pre[:], in_=hid[t][:], func=ACT.Copy, scale=unit_sb[:, t : t + 1])
-            scaled[t] = pre
-
-        def update_gate(t):
-            pre = plane("gate_pre", t)
-            nc.vector.scalar_tensor_tensor(
-                out=pre[:], in0=hid[t][:], scalar=vu_sb[:, t : t + 1], in1=product("wu", t)[:], op0=ALU.mult, op1=ALU.add
-            )
-            gate_t[t] = plane("gate_t", t)
-            nc.scalar.activation(out=gate_t[t][:], in_=turned("gate_pre_t%d" % t, "pre", pre)[:], func=ACT.Sigmoid)
-
-        def keep_term(t):
-            nc.vector.scalar_tensor_tensor(
-                out=kept[:, t, :], in0=size[t][:], scalar=0.3, in1=scaled[t][:], op0=ALU.add, op1=ALU.mult
-            )
+            nc.scalar.activation(out=neg_cand[t][:], in_=cand_pre[:], func=ACT.Tanh, scale=-1.0)
+            if t in STATE_ON_TENSOR:
+                neg_hid_t[t] = plane("neg_hid_t", t)
+                nc.scalar.activation(
+                    out=neg_hid_t[t][:], in_=turned("hid_t%d" % t, "pre", hid[t])[:], func=ACT.Copy, scale=-1.0
+                )
 
         def step(t):
+            gate_pre = plane("gate_pre", t)
+            nc.vector.scalar_tensor_tensor(
+                out=gate_pre[:],
+                in0=hid[t][:],
+                scalar=vu_sb[:, t : t + 1],
+                in1=product("wu", t)[:],
+                op0=ALU.mult,
+                op1=ALU.add,
+            )
+            gate_t[t] = plane("gate_t", t)
+            nc.scalar.activation(out=gate_t[t][:], in_=turned("gate_pre_t%d" % t, "pre", gate_pre)[:], func=ACT.Sigmoid)
+            diff_t[t] = turned("diff_t%d" % t, "diff", hid[t], neg_cand[t])
             step_t[t] = plane("step_t", t)
             for s in range(S // P):
                 cols = slice(P * s, P * (s + 1))
@@ -185,105 +179,93 @@ def tile_picked_yaugru_mix_p_kernel(
                     op1=ALU.mult,
                 )
 
-        def move_term(t):
+        def moved_term(t):
+            size[t] = plane("size", t)
+            nc.scalar.activation(out=size[t][:], in_=neg_cand[t][:], func=ACT.Abs)
+            terms = (step_t[t], neg_hid_t[t]) if t in STATE_ON_TENSOR else (step_t[t],)
             nc.vector.scalar_tensor_tensor(
                 out=moved[:, t, :],
-                in0=turned("step%d" % t, "cand", step_t[t])[:],
+                in0=turned("step%d" % t, "cand", *terms)[:],
                 scalar=unit_sb[:, t : t + 1],
                 in1=size[t][:],
                 op0=ALU.mult,
                 op1=ALU.mult,
             )
 
-        def cast_readout():
-            grouped["wo"] = tenant(7, [P, N, PACK], BF16, "grouped_wo")
+        def kept_term(t):
+            if t in STATE_ON_TENSOR:
+                nc.scalar.activation(out=kept[:, t, :], in_=hid[t][:], func=ACT.Copy, scale=unit_03[:, t : t + 1])
+            else:
+                unit_hid = reset[t]
+                nc.scalar.activation(out=unit_hid[:], in_=hid[t][:], func=ACT.Copy, scale=unit_sb[:, t : t + 1])
+                nc.vector.scalar_tensor_tensor(
+                    out=kept[:, t, :], in0=size[t][:], scalar=0.3, in1=unit_hid[:], op0=ALU.add, op1=ALU.mult
+                )
+
+        def quantize_readout():
+            rounded["wo"] = aligned([P, N, PACK], BF16, "rounded_wo")
             nc.scalar.copy(
-                out=grouped["wo"][:].rearrange("p (c i) j -> p c j i", i=4),
+                out=rounded["wo"][:].rearrange("p (c i) j -> p c j i", i=4),
                 in_=raw_wo[:].rearrange("p j (c i) -> p c j i", i=4),
             )
+            quantize("wo", rounded["wo"][:].rearrange("p n j -> p (n j)"), N)
 
         zz = {}
+        chunk_cols = [slice(sum(CHUNKS[:c]), sum(CHUNKS[: c + 1])) for c in range(len(CHUNKS))]
 
         def mix(c):
-            cols = slice(CHUNK * c, CHUNK * (c + 1))
-            zz[c] = keep.tile([P, CHUNK, PACK], BF16, name="zz%d" % c, align_bytes=64)
+            zz[c] = aligned([P, CHUNKS[c], PACK], BF16, "zz%d" % c)
             nc.vector.tensor_tensor(
                 out=zz[c][:].rearrange("p (c i) t -> p c t i", i=4),
-                in0=kept[:, :, cols].rearrange("p t (c i) -> p c t i", i=4),
-                in1=moved[:, :, cols].rearrange("p t (c i) -> p c t i", i=4),
+                in0=kept[:, :, chunk_cols[c]].rearrange("p t (c i) -> p c t i", i=4),
+                in1=moved[:, :, chunk_cols[c]].rearrange("p t (c i) -> p c t i", i=4),
                 op=ALU.subtract,
             )
 
         out_rows = out.rearrange("(a p) j -> p a j", p=P)
 
         def read_out(c):
-            name = "zz%d" % c
-            quantize(name, zz[c][:].rearrange("p n t -> p (n t)"), CHUNK)
-            bank = psum.tile([P, N // P, CHUNK], F32, name="out%d" % c, tag="gate", bufs=2)
+            key = "zz%d" % c
+            quantize(key, zz[c][:].rearrange("p n t -> p (n t)"), CHUNKS[c])
+            bank = psum.tile([P, N // P, CHUNKS[c]], F32, name="out%d" % c, tag=("gate", "diff")[c % 2], bufs=2)
             for a in range(N // P):
                 cols = slice(P * a, P * (a + 1))
                 nc.tensor.matmul_mx(
                     out=bank[:, a, :],
                     lhsT=codes["wo"][:, cols].bitcast(FP8X4),
                     lhsT_scale=scales["wo"][:, cols],
-                    rhs=codes[name][:].bitcast(FP8X4),
-                    rhs_scale=scales[name][:],
+                    rhs=codes[key][:].bitcast(FP8X4),
+                    rhs_scale=scales[key][:],
                     start=True,
                     stop=True,
                 )
-            result = keep.tile([P, N // P, CHUNK], F32, name="result%d" % c)
+            result = sbuf.tile([P, N // P, CHUNKS[c]], F32, name="result%d" % c)
             nc.scalar.copy(out=result[:], in_=bank[:])
-            nc.sync.dma_start(out=out_rows[:, :, CHUNK * c : CHUNK * (c + 1)], in_=result[:])
+            nc.sync.dma_start(out=out_rows[:, :, chunk_cols[c]], in_=result[:])
 
-        cast_weight("wr", 0, nc.vector.tensor_copy, 0)
-        cast_weight("wr", 1, nc.scalar.copy, None)
-        quantize_weight("wr", 0)
-        quantize_weight("wr", 1)
-        reset_gate(0)
-        reset_gate(1)
-        gather_state(0)
-        gate_state(0)
-        cast_weight("wh", 0, nc.vector.tensor_copy, 1)
-        cast_weight("wh", 1, nc.scalar.copy, 2)
-        reset_gate(2)
-        reset_gate(3)
-        quantize_weight("wh", 0)
-        quantize_weight("wh", 1)
-        gather_state(1)
-        cast_weight("wu", 0, nc.scalar.copy, 3)
-        candidate(0)
-        cast_weight("wu", 1, nc.scalar.copy, 4)
-        gate_state(1)
-        candidate(1)
-        gather_state(2)
-        quantize_weight("wu", 0)
-        gate_state(2)
-        quantize_weight("wu", 1)
-        candidate(2)
-        update_gate(0)
-        gather_state(3)
-        update_gate(1)
-        gate_state(3)
-        keep_term(0)
-        candidate(3)
-        step(0)
-        update_gate(2)
-        keep_term(1)
-        step(1)
-        update_gate(3)
-        cast_readout()
-        move_term(0)
-        keep_term(2)
-        step(2)
-        move_term(1)
-        step(3)
-        keep_term(3)
-        move_term(2)
-        quantize("wo", grouped["wo"][:].rearrange("p n j -> p (n j)"), N)
-        move_term(3)
-        chunks = S // CHUNK
+        for name, copies in (
+            ("wr", (nc.vector.tensor_copy, nc.vector.tensor_copy)),
+            ("wh", (nc.vector.tensor_copy, nc.scalar.copy)),
+            ("wu", (nc.scalar.copy, nc.scalar.copy)),
+        ):
+            for half in range(2):
+                round_weight(name, half, copies[half])
+            for half in range(2):
+                quantize_weight(name, half)
+            if name == "wr":
+                for t in range(PACK):
+                    reset_gate(t)
+
+        for turn in range(PACK + 3):
+            for stage, lag in ((candidate, 0), (step, 2), (moved_term, 3)):
+                if 0 <= turn - lag < PACK:
+                    stage(turn - lag)
+        for t in range(PACK):
+            kept_term(t)
+        quantize_readout()
+
         mix(0)
-        for c in range(chunks):
-            if c + 1 < chunks:
+        for c in range(len(CHUNKS)):
+            if c + 1 < len(CHUNKS):
                 mix(c + 1)
             read_out(c)

from contextlib import ExitStack

import concourse.mybir as mybir
from concourse.masks import make_identity

K, T, S, N, H, U = 512, 1024, 512, 256, 512, 1024
P = 128
PACK = 4
FLOPS = 2 * K * H * S * 3 + 2 * H * N * S

F32 = mybir.dt.float32
BF16 = mybir.dt.bfloat16
I32 = mybir.dt.int32
U32 = mybir.dt.uint32
U16 = mybir.dt.uint16
U8 = mybir.dt.uint8
FP8X4 = mybir.dt.float8_e4m3fn_x4
ALU = mybir.AluOpType
ACT = mybir.ActivationFunctionType

CHUNKS = (128, 128, 128, 64, 64)
STATE_ON_TENSOR = (1, 2)


def tile_picked_yaugru_mix_p_kernel(
    tc, x_words, x_scales, wu, wr, wh, mem, att, vu, vh, unit, wo, offs, user, out
):
    nc = tc.nc
    with ExitStack() as ctx:
        sbuf = ctx.enter_context(tc.tile_pool(name="sbuf", bufs=1))
        psum = ctx.enter_context(tc.psum_pool(name="psum", bufs=1))

        def aligned(shape, dtype, name):
            return sbuf.tile(shape, dtype, name=name, align_bytes=64)

        offs_sb = sbuf.tile([P, S // 16], U16, name="offs_sb")
        user_sb = sbuf.tile([P, S // 16], U16, name="user_sb")
        words_all = sbuf.tile([P, T], I32, name="words_all")
        bytes_all = sbuf.tile([P, T], U8, name="bytes_all")
        raw = {name: sbuf.tile([P, PACK, H], F32, name="raw_" + name) for name in ("wr", "wh", "wu")}
        raw_wo = sbuf.tile([P, PACK, N], F32, name="raw_wo")
        mem_sb = [aligned([P, U], F32, "mem%d" % t) for t in range(PACK)]
        vu_sb = sbuf.tile([P, PACK], F32, name="vu_sb")
        vh_sb = sbuf.tile([P, PACK], F32, name="vh_sb")
        unit_sb = sbuf.tile([P, PACK], F32, name="unit_sb")
        att_sb = sbuf.tile([P, S // P], F32, name="att_sb")
        ident = sbuf.tile([P, P], F32, name="ident")

        mem_rows = mem.rearrange("(p t) u -> p t u", t=PACK)

        def four_rows(w):
            return w.rearrange("(p j) c -> p j c", j=PACK)

        def by_plane(v):
            return v.rearrange("(p t) o -> p (t o)", t=PACK)

        nc.vector.memset(bytes_all[:].bitcast(I32), 0)
        nc.sync.dma_start(out=words_all[:], in_=x_words[0].rearrange("p c r -> p (c r)").bitcast(I32))
        nc.sync.dma_start(offs_sb[:], offs)
        for q in range(P // 32):
            nc.sync.dma_start(
                out=bytes_all[32 * q : 32 * q + 4, :].bitcast(I32), in_=x_scales[0, 4 * q : 4 * q + 4, :].bitcast(I32)
            )
        nc.sync.dma_start(out=raw["wr"][:], in_=four_rows(wr))
        nc.sync.dma_start(user_sb[:], user)
        nc.sync.dma_start(out=mem_sb[0][:], in_=mem_rows[:, 0, :])
        nc.sync.dma_start(out=raw["wh"][:], in_=four_rows(wh))
        nc.sync.dma_start(out=mem_sb[1][:], in_=mem_rows[:, 1, :])
        nc.sync.dma_start(out=raw["wu"][:], in_=four_rows(wu))
        nc.sync.dma_start(out=mem_sb[2][:], in_=mem_rows[:, 2, :])
        nc.sync.dma_start(out=mem_sb[3][:], in_=mem_rows[:, 3, :])
        with nc.allow_non_contiguous_dma(reason="one attention value a partition"):
            nc.sync.dma_start(out=att_sb[:], in_=att[0:1, :].rearrange("o (s p) -> p (o s)", p=P))
        nc.sync.dma_start(out=raw_wo[:], in_=four_rows(wo))
        nc.gpsimd.dma_start(out=vh_sb[:], in_=by_plane(vh))
        nc.gpsimd.dma_start(out=unit_sb[:], in_=by_plane(unit))
        nc.gpsimd.dma_start(out=vu_sb[:], in_=by_plane(vu))
        make_identity(nc, ident[:])
        unit_03 = sbuf.tile([P, PACK], F32, name="unit_03")
        nc.gpsimd.tensor_scalar(out=unit_03[:], in0=unit_sb[:], scalar1=0.3, scalar2=None, op0=ALU.mult)

        x_codes = aligned([P, S], U32, "x_codes")
        x_scale = aligned([P, S], U8, "x_scale")
        nc.vector.tensor_copy(out=x_codes[:], in_=words_all[:].bitcast(U32).indirect(offs_sb[:]))
        nc.vector.tensor_copy(out=x_scale[:], in_=bytes_all[:].indirect(offs_sb[:]))

        rounded, codes, scales = {}, {}, {}

        def round_weight(name, half, copy):
            key = "%s%d" % (name, half)
            rounded[key] = aligned([P, 2, P, PACK], BF16, "rounded_" + key)
            src = raw[name][:].rearrange("p j (m t) -> p m j t", t=PACK)
            copy(out=rounded[key][:].rearrange("p t m j -> p m j t"), in_=src[:, :, :, 2 * half : 2 * half + 2])

        def quantize(key, flat, width):
            codes[key] = aligned([P, width], U32, "codes_" + key)
            scales[key] = aligned([P, width], U8, "scales_" + key)
            nc.vector.quantize_mx(out=codes[key][:].bitcast(FP8X4), scales=scales[key][:], in_=flat)

        def quantize_weight(name, half):
            key = "%s%d" % (name, half)
            quantize(key, rounded[key][:].rearrange("p t m j -> p (t m j)"), H // 2)

        def product(name, t):
            bank = psum.tile([P, S], F32, name="y_%s%d" % (name, t), tag="cand" if name == "wh" else "gate", bufs=2)
            key = "%s%d" % (name, t // 2)
            cols = slice(P * (t % 2), P * (t % 2 + 1))
            nc.tensor.matmul_mx(
                out=bank[:],
                lhsT=codes[key][:, cols].bitcast(FP8X4),
                lhsT_scale=scales[key][:, cols],
                rhs=x_codes[:].bitcast(FP8X4),
                rhs_scale=x_scale[:],
                start=True,
                stop=True,
            )
            return bank

        def turned(name, tag, *terms):
            bank = psum.tile([P, S], F32, name=name, tag=tag, bufs=2)
            for s in range(S // P):
                cols = slice(P * s, P * (s + 1))
                for n, term in enumerate(terms):
                    nc.tensor.matmul(
                        bank[:, cols], term[:, cols], ident[:], start=(n == 0), stop=(n == len(terms) - 1), is_transpose=True
                    )
            return bank

        def plane(name, t):
            return aligned([P, S], F32, "%s%d" % (name, t))

        hid, reset, gated, neg_cand, size, diff_t, gate_t, step_t, neg_hid_t = {}, {}, {}, {}, {}, {}, {}, {}, {}
        kept = sbuf.tile([P, PACK, S], F32, name="kept")
        moved = sbuf.tile([P, PACK, S], F32, name="moved")

        def reset_gate(t):
            reset[t] = plane("reset", t)
            nc.scalar.activation(out=reset[t][:], in_=product("wr", t)[:], func=ACT.Sigmoid)

        def candidate(t):
            hid[t] = plane("hid", t)
            nc.vector.tensor_copy(out=hid[t][:], in_=mem_sb[t][:].indirect(user_sb[:]))
            gated[t] = plane("gated", t)
            nc.vector.scalar_tensor_tensor(
                out=gated[t][:], in0=hid[t][:], scalar=vh_sb[:, t : t + 1], in1=reset[t][:], op0=ALU.mult, op1=ALU.mult
            )
            cand_pre = plane("cand_pre", t)
            nc.vector.tensor_tensor(out=cand_pre[:], in0=product("wh", t)[:], in1=gated[t][:], op=ALU.add)
            neg_cand[t] = plane("neg_cand", t)
            nc.scalar.activation(out=neg_cand[t][:], in_=cand_pre[:], func=ACT.Tanh, scale=-1.0)
            if t in STATE_ON_TENSOR:
                neg_hid_t[t] = plane("neg_hid_t", t)
                nc.scalar.activation(
                    out=neg_hid_t[t][:], in_=turned("hid_t%d" % t, "pre", hid[t])[:], func=ACT.Copy, scale=-1.0
                )

        def step(t):
            gate_pre = plane("gate_pre", t)
            nc.vector.scalar_tensor_tensor(
                out=gate_pre[:],
                in0=hid[t][:],
                scalar=vu_sb[:, t : t + 1],
                in1=product("wu", t)[:],
                op0=ALU.mult,
                op1=ALU.add,
            )
            gate_t[t] = plane("gate_t", t)
            nc.scalar.activation(out=gate_t[t][:], in_=turned("gate_pre_t%d" % t, "pre", gate_pre)[:], func=ACT.Sigmoid)
            diff_t[t] = turned("diff_t%d" % t, "diff", hid[t], neg_cand[t])
            step_t[t] = plane("step_t", t)
            for s in range(S // P):
                cols = slice(P * s, P * (s + 1))
                nc.vector.scalar_tensor_tensor(
                    out=step_t[t][:, cols],
                    in0=gate_t[t][:, cols],
                    scalar=att_sb[:, s : s + 1],
                    in1=diff_t[t][:, cols],
                    op0=ALU.mult,
                    op1=ALU.mult,
                )

        def moved_term(t):
            size[t] = plane("size", t)
            nc.scalar.activation(out=size[t][:], in_=neg_cand[t][:], func=ACT.Abs)
            terms = (step_t[t], neg_hid_t[t]) if t in STATE_ON_TENSOR else (step_t[t],)
            nc.vector.scalar_tensor_tensor(
                out=moved[:, t, :],
                in0=turned("step%d" % t, "cand", *terms)[:],
                scalar=unit_sb[:, t : t + 1],
                in1=size[t][:],
                op0=ALU.mult,
                op1=ALU.mult,
            )

        def kept_term(t):
            if t in STATE_ON_TENSOR:
                nc.scalar.activation(out=kept[:, t, :], in_=hid[t][:], func=ACT.Copy, scale=unit_03[:, t : t + 1])
            else:
                unit_hid = reset[t]
                nc.scalar.activation(out=unit_hid[:], in_=hid[t][:], func=ACT.Copy, scale=unit_sb[:, t : t + 1])
                nc.vector.scalar_tensor_tensor(
                    out=kept[:, t, :], in0=size[t][:], scalar=0.3, in1=unit_hid[:], op0=ALU.add, op1=ALU.mult
                )

        def quantize_readout():
            rounded["wo"] = aligned([P, N, PACK], BF16, "rounded_wo")
            nc.scalar.copy(
                out=rounded["wo"][:].rearrange("p (c i) j -> p c j i", i=4),
                in_=raw_wo[:].rearrange("p j (c i) -> p c j i", i=4),
            )
            quantize("wo", rounded["wo"][:].rearrange("p n j -> p (n j)"), N)

        zz = {}
        chunk_cols = [slice(sum(CHUNKS[:c]), sum(CHUNKS[: c + 1])) for c in range(len(CHUNKS))]

        def mix(c):
            zz[c] = aligned([P, CHUNKS[c], PACK], BF16, "zz%d" % c)
            nc.vector.tensor_tensor(
                out=zz[c][:].rearrange("p (c i) t -> p c t i", i=4),
                in0=kept[:, :, chunk_cols[c]].rearrange("p t (c i) -> p c t i", i=4),
                in1=moved[:, :, chunk_cols[c]].rearrange("p t (c i) -> p c t i", i=4),
                op=ALU.subtract,
            )

        out_rows = out.rearrange("(a p) j -> p a j", p=P)

        def read_out(c):
            key = "zz%d" % c
            quantize(key, zz[c][:].rearrange("p n t -> p (n t)"), CHUNKS[c])
            bank = psum.tile([P, N // P, CHUNKS[c]], F32, name="out%d" % c, tag=("gate", "diff")[c % 2], bufs=2)
            for a in range(N // P):
                cols = slice(P * a, P * (a + 1))
                nc.tensor.matmul_mx(
                    out=bank[:, a, :],
                    lhsT=codes["wo"][:, cols].bitcast(FP8X4),
                    lhsT_scale=scales["wo"][:, cols],
                    rhs=codes[key][:].bitcast(FP8X4),
                    rhs_scale=scales[key][:],
                    start=True,
                    stop=True,
                )
            result = sbuf.tile([P, N // P, CHUNKS[c]], F32, name="result%d" % c)
            nc.scalar.copy(out=result[:], in_=bank[:])
            nc.sync.dma_start(out=out_rows[:, :, chunk_cols[c]], in_=result[:])

        for name, copies in (
            ("wr", (nc.vector.tensor_copy, nc.vector.tensor_copy)),
            ("wh", (nc.vector.tensor_copy, nc.scalar.copy)),
            ("wu", (nc.scalar.copy, nc.scalar.copy)),
        ):
            for half in range(2):
                round_weight(name, half, copies[half])
            for half in range(2):
                quantize_weight(name, half)
            if name == "wr":
                for t in range(PACK):
                    reset_gate(t)

        for turn in range(PACK + 3):
            for stage, lag in ((candidate, 0), (step, 2), (moved_term, 3)):
                if 0 <= turn - lag < PACK:
                    stage(turn - lag)
        for t in range(PACK):
            kept_term(t)
        quantize_readout()

        mix(0)
        for c in range(len(CHUNKS)):
            if c + 1 < len(CHUNKS):
                mix(c + 1)
            read_out(c)
